import numpy as np
import ml_dtypes


def mxq(x, axis, fmt="e4m3"):
    dtype, down = {"e4m3": (ml_dtypes.float8_e4m3fn, 7), "e5m2": (ml_dtypes.float8_e5m2, 14)}[fmt]
    v = np.moveaxis(np.asarray(x, np.float32).astype(ml_dtypes.bfloat16).astype(np.float64), axis, -1)
    blocks = v.reshape(v.shape[:-1] + (-1, 32))
    amax = np.abs(blocks).max(-1, keepdims=True)
    byte = np.maximum(np.where(amax > 0, np.frexp(amax)[1] - 1 + 127, 0) - down, 1)
    scale = np.exp2(byte - 127.0)
    codes = (blocks / scale).astype(np.float32).astype(dtype).astype(np.float64)
    return np.moveaxis((codes * scale).reshape(v.shape), -1, axis)


WIDE = False


def mx_kscale(k):
    if not WIDE:
        return np.ones(k)
    levels = np.array([10, -10, 5, -5, 0])
    if k % 512:
        return np.exp2(np.random.permutation(np.resize(levels, k // 32))).repeat(32)
    a = np.empty((k // 512, 16))
    for p in range(k // 512):
        a[p, :8] = np.random.permutation(np.resize(levels, 8))
        for g in range(8):
            far = levels[np.abs(levels - a[p, g]) >= 10]
            a[p, g + 8] = far[np.random.randint(len(far))]
    return np.exp2(a.ravel()).repeat(32)


def f64(x):
    return np.asarray(x).astype(np.float64)


def striped(idx):
    return np.tile(np.asarray(idx).reshape(-1, 16).T, (8, 1)).astype(np.uint16)


def unstriped(offs):
    return offs[:16].T.reshape(-1).astype(np.int64)


def striped8(idx):
    return np.asarray(idx).reshape(8, -1, 16).transpose(0, 2, 1).reshape(128, -1).astype(np.uint16)


def unstriped8(offs):
    return offs.reshape(8, 16, -1).transpose(0, 2, 1).reshape(8, -1).astype(np.int64)


def pick8(x, idx, run):
    r = np.arange(len(x))
    return x[r[:, None], idx[r % (8 * run) // run]]


E2M1 = np.array([0.0, 0.5, 1.0, 1.5, 2.0, 3.0, 4.0, 6.0, -0.0, -0.5, -1.0, -1.5, -2.0, -3.0, -4.0, -6.0])


def pack_weight(w, fmt):
    k, n = w.shape
    w = f64(np.asarray(w, np.float32).astype(ml_dtypes.bfloat16)).reshape(k // 32, 32, n)
    amax = np.abs(w).max(1)
    if fmt == "e4m3":
        byte = np.frexp(amax)[1] - 1 + 127 - 7
    else:
        mant, ex = np.frexp(amax / 6.0)
        byte = np.where(mant > 0.5, ex, ex - 1) + 127
    byte = np.clip(np.where(amax > 0, byte, 1), 1, 254)
    scaled = (w * np.exp2(127.0 - byte)[:, None, :]).reshape(k, n).astype(np.float32)
    by_word = np.ascontiguousarray(scaled.reshape(k // 512, 128, 4, n).transpose(0, 1, 3, 2))
    if fmt == "e4m3":
        words = by_word.astype(ml_dtypes.float8_e4m3fn).view(np.uint8)
    else:
        c = by_word.astype(ml_dtypes.float4_e2m1fn).view(np.uint8) & 0xF
        words = (c[..., 0::2] | (c[..., 1::2] << 4)).reshape(k // 512, 128, 2 * n)
    return np.ascontiguousarray(words), np.ascontiguousarray(byte.astype(np.uint8).reshape(k // 512, 16, n))


def unpack_weight(words, scales, fmt):
    g, _, n = scales.shape
    words = np.ascontiguousarray(words).reshape(g, 128, n, -1)
    if fmt == "e4m3":
        vals = words.view(ml_dtypes.float8_e4m3fn).astype(np.float64)
    else:
        nib = np.empty((g, 128, n, 4), np.uint8)
        nib[..., 0::2] = words & 0xF
        nib[..., 1::2] = words >> 4
        vals = E2M1[nib]
    vals = vals * np.repeat(np.exp2(scales.astype(np.float64) - 127.0), 8, axis=1)[..., None]
    return vals.transpose(0, 1, 3, 2).reshape(g * 512, n)


K, J, R, T, Z, M, C, O, N = 512, 256, 512, 1024, 512, 1024, 512, 128, 256


def setup_inputs():
    n = np.random.standard_normal
    idx = np.random.permutation(T)[:J]
    idx2 = np.random.permutation(M)[:J]
    idx3 = np.stack([np.random.permutation(C)[:J] for _ in range(8)])
    idx4 = np.stack([np.random.permutation(C)[:J] for _ in range(8)])
    idx5 = np.stack([np.random.permutation(C)[:O] for _ in range(8)])
    idx6 = np.stack([np.random.permutation(C)[:O] for _ in range(8)])
    fk = mx_kscale(K)
    fr = mx_kscale(R)
    fz = mx_kscale(Z)
    xtp = pack_weight(n((K, T)) * fk[:, None], "e2m1")
    wp = pack_weight(n((K, R)) * 1 / np.sqrt(K) / fk[:, None] * fr, "e4m3")
    xop = pack_weight(n((Z, M)) / fz[:, None], "e4m3")
    w2p = pack_weight(n((Z, R)) * 1 / np.sqrt(Z) * fz[:, None] * fr, "e2m1")
    wbp = pack_weight(n((R, N)) * 1 / np.sqrt(R) / fr[:, None], "e2m1")
    return {
        "xt_words": xtp[0],
        "xt_scales": xtp[1],
        "w_words": wp[0],
        "w_scales": wp[1],
        "xo_words": xop[0],
        "xo_scales": xop[1],
        "w2_words": w2p[0],
        "w2_scales": w2p[1],
        "sa": (np.random.uniform(0.5, 1.6, (R, 1))).astype(np.float32),
        "sb": (np.random.uniform(0.5, 1.6, (R, 1))).astype(np.float32),
        "wb_words": wbp[0],
        "wb_scales": wbp[1],
        "offs": striped(idx),
        "offs2": striped(idx2),
        "offs3": striped8(idx3),
        "offs4": striped8(idx4),
        "offs5": striped8(idx5),
        "offs6": striped8(idx6),
    }


def reference(xt_words, xt_scales, w_words, w_scales, xo_words, xo_scales, w2_words, w2_scales, sa, sb, wb_words, wb_scales, offs, offs2, offs3, offs4, offs5, offs6):
    idx = unstriped(offs)
    idx2 = unstriped(offs2)
    idx3 = unstriped8(offs3)
    idx4 = unstriped8(offs4)
    idx5 = unstriped8(offs5)
    idx6 = unstriped8(offs6)
    xtu = unpack_weight(xt_words, xt_scales, "e2m1")
    wu = unpack_weight(w_words, w_scales, "e4m3")
    xou = unpack_weight(xo_words, xo_scales, "e4m3")
    w2u = unpack_weight(w2_words, w2_scales, "e2m1")
    wbu = unpack_weight(wb_words, wb_scales, "e2m1")
    xtidxg = xtu[:, idx]
    a = wu.T @ xtidxg
    xoidx2g = xou[:, idx2]
    b = w2u.T @ xoidx2g
    pw = np.zeros((R, C))
    pw[np.arange(R)[:, None], idx3[np.arange(R) % 512 // 64]] = a
    pv = np.zeros((R, C))
    pv[np.arange(R)[:, None], idx4[np.arange(R) % 512 // 64]] = b
    g1 = np.pad(pv, ((0, 0), (1, 0)))[:, :C]
    ph = np.maximum(pw, g1)
    g2 = np.pad(pw, ((0, 0), (1, 0)))[:, :C]
    pl = np.minimum(pv, g2)
    hid = pick8(ph, idx5, 64) * f64(sa) - pick8(pl, idx6, 64) * f64(sb)
    hidq = mxq(hid, 0, "e4m3")
    y = wbu.T @ hidq
    return y

@@ -1,0 +1,163 @@
+from contextlib import ExitStack
+
+import concourse.mybir as mybir
+
+K, J, R, T, Z, M, C, O, N = 512, 256, 512, 1024, 512, 1024, 512, 128, 256
+FLOPS = 2 * (K * R * J + Z * R * J + R * N * O)
+
+F32 = mybir.dt.float32
+BF16 = mybir.dt.bfloat16
+I32 = mybir.dt.int32
+U32 = mybir.dt.uint32
+U16 = mybir.dt.uint16
+U8 = mybir.dt.uint8
+FP8X4 = mybir.dt.float8_e4m3fn_x4
+FP4X4 = mybir.dt.float4_e2m1fn_x4
+COPY = mybir.ActivationFunctionType.Copy
+ALU = mybir.AluOpType
+
+P = 128
+PACK = 4
+QUADS = 4
+
+
+def tile_picked_tokens_plain_two_staggered_one_plain_kernel(
+    tc, xt_words, xt_scales, w_words, w_scales, xo_words, xo_scales, w2_words, w2_scales,
+    sa, sb, wb_words, wb_scales, offs, offs2, offs3, offs4, offs5, offs6, out,
+):
+    nc = tc.nc
+    with ExitStack() as ctx:
+        keep = ctx.enter_context(tc.tile_pool(name="keep", bufs=1))
+        psum = ctx.enter_context(tc.psum_pool(name="psum", bufs=4))
+        psum_out = ctx.enter_context(tc.psum_pool(name="psum_out", bufs=2))
+
+        def sbuf(name, shape, dtype, tag=None):
+            return keep.tile(shape, dtype, name=name, tag=tag or name, align_bytes=64)
+
+        def load_list(name, src):
+            tile = sbuf(name, list(src.shape), U16)
+            nc.sync.dma_start(tile[:], src)
+            return tile
+
+        def load_words(name, src, cols, dtype):
+            tile = sbuf(name, [P, cols], dtype)
+            nc.sync.dma_start(tile[:].bitcast(I32), src.bitcast(I32))
+            return tile
+
+        def scale_plane(name, cols):
+            tile = sbuf(name, [P, cols], U8)
+            nc.vector.memset(tile[:].bitcast(I32), 0)
+            return tile
+
+        def load_scales(plane, src):
+            rows = src[0].bitcast(I32)
+            for q in range(QUADS):
+                nc.sync.dma_start(plane[32 * q : 32 * q + 4, :].bitcast(I32), rows[4 * q : 4 * q + 4, :])
+
+        xt_plane = scale_plane("xt_plane", T)
+        w_plane = scale_plane("w_plane", R)
+
+        put_a_list = load_list("put_a_list", offs3)
+        tok_list = load_list("tok_list", offs)
+        xt_table = load_words("xt_table", xt_words[0], T, U16)
+        w_raw = load_words("w_raw", w_words[0].rearrange("p n t -> p (n t)"), R, I32)
+        load_scales(xt_plane, xt_scales)
+        load_scales(w_plane, w_scales)
+
+        board_w = [sbuf("board_w%d" % t, [P, C], F32) for t in range(PACK)]
+        for t in range(PACK):
+            nc.vector.memset(board_w[t][:], 0.0)
+
+        xo_plane = scale_plane("xo_plane", M)
+        w2_plane = scale_plane("w2_plane", R)
+        wb_plane = sbuf("wb_plane", [P, N], U8)
+        note_list = load_list("note_list", offs2)
+        xo_table = load_words("xo_table", xo_words[0].rearrange("p n t -> p (n t)"), M, U32)
+        load_scales(xo_plane, xo_scales)
+        w2_raw = load_words("w2_raw", w2_words[0], R, U16)
+        load_scales(w2_plane, w2_scales)
+        put_b_list = load_list("put_b_list", offs4)
+        sa_cols = sbuf("sa_cols", [P, PACK], F32)
+        sb_cols = sbuf("sb_cols", [P, PACK], F32)
+        nc.sync.dma_start(sa_cols[:], sa.rearrange("(p t) o -> p (t o)", t=PACK))
+        nc.sync.dma_start(sb_cols[:], sb.rearrange("(p t) o -> p (t o)", t=PACK))
+        get_hi_list = load_list("get_hi_list", offs5)
+        get_lo_list = load_list("get_lo_list", offs6)
+        wb_codes = load_words("wb_codes", wb_words[0], N, U16)
+        load_scales(wb_plane, wb_scales)
+
+        w_codes = sbuf("w_codes", [P, PACK, P], I32)
+        w_bytes = sbuf("w_bytes", [P, PACK, P], U8)
+        xt_codes = sbuf("xt_codes", [P, J], U16)
+        xt_bytes = sbuf("xt_bytes", [P, J], U8)
+
+        def deal(dst, src, t0, t1):
+            nc.vector.tensor_copy(dst[:, t0:t1, :], src[:].rearrange("p (m t) -> p t m", t=PACK)[:, t0:t1, :])
+
+        nc.vector.tensor_copy(xt_bytes[:], xt_plane[:].indirect(tok_list[:]))
+        nc.vector.tensor_copy(xt_codes[:], xt_table[:].indirect(tok_list[:]))
+        deal(w_codes, w_raw, 0, 1)
+        deal(w_bytes, w_plane, 0, 1)
+
+        def product_to_board(name, codes, scales, moving, moving_scales, board, put_list):
+            acc = psum.tile([P, J], F32, name="acc")
+            nc.tensor.matmul_mx(out=acc[:], lhsT=codes, lhsT_scale=scales, rhs=moving,
+                                rhs_scale=moving_scales, start=True, stop=True)
+            res = sbuf(name, [P, J], F32)
+            nc.vector.tensor_copy(res[:], acc[:])
+            nc.scalar.activation(board[:].indirect(put_list[:]), res[:], COPY)
+
+        for t in range(PACK):
+            product_to_board("a%d" % t, w_codes[:, t, :].bitcast(FP8X4), w_bytes[:, t, :],
+                             xt_codes[:].bitcast(FP4X4), xt_bytes[:], board_w[t], put_a_list)
+            if t == 0:
+                deal(w_bytes, w_plane, 1, PACK)
+                deal(w_codes, w_raw, 1, PACK)
+
+        xo_codes = sbuf("xo_codes", [P, J], U32)
+        xo_bytes = sbuf("xo_bytes", [P, J], U8)
+        w2_codes = sbuf("w2_codes", [P, PACK, P], U16)
+        w2_bytes = sbuf("w2_bytes", [P, PACK, P], U8)
+        nc.vector.tensor_copy(xo_codes[:], xo_table[:].indirect(note_list[:]))
+        nc.vector.tensor_copy(xo_bytes[:], xo_plane[:].indirect(note_list[:]))
+        deal(w2_codes, w2_raw, 0, PACK)
+        deal(w2_bytes, w2_plane, 0, PACK)
+        board_v = [sbuf("board_v%d" % t, [P, C], F32, tag="a%d" % t) for t in range(PACK)]
+        for t in range(PACK):
+            nc.gpsimd.memset(board_v[t][:], 0.0)
+            product_to_board("b%d" % t, w2_codes[:, t, :].bitcast(FP4X4), w2_bytes[:, t, :],
+                             xo_codes[:].bitcast(FP8X4), xo_bytes[:], board_v[t], put_b_list)
+
+        hid = sbuf("hid", [P, O, PACK], BF16)
+        fetched = []
+        for t in range(PACK):
+            upper = sbuf("upper%d" % t, [P, C], F32)
+            lower = sbuf("lower%d" % t, [P, C], F32)
+            nc.vector.tensor_scalar(upper[:, 0:1], board_w[t][:, 0:1], 0.0, None, ALU.max)
+            nc.vector.tensor_tensor(upper[:, 1:C], board_w[t][:, 1:C], board_v[t][:, 0 : C - 1], ALU.max)
+            nc.vector.tensor_scalar(lower[:, 0:1], board_v[t][:, 0:1], 0.0, None, ALU.min)
+            nc.vector.tensor_tensor(lower[:, 1:C], board_v[t][:, 1:C], board_w[t][:, 0 : C - 1], ALU.min)
+            hi = sbuf("hi%d" % t, [P, O], F32)
+            lo = sbuf("lo%d" % t, [P, O], F32)
+            nc.scalar.activation(hi[:], upper[:].indirect(get_hi_list[:]), COPY, scale=sa_cols[:, t : t + 1])
+            nc.scalar.activation(lo[:], lower[:].indirect(get_lo_list[:]), COPY, scale=sb_cols[:, t : t + 1])
+            fetched.append((hi, lo))
+        for t, (hi, lo) in enumerate(fetched):
+            nc.vector.tensor_tensor(hid[:, :, t], hi[:], lo[:], ALU.subtract)
+
+        hid_codes = sbuf("hid_codes", [P, O], U32)
+        hid_bytes = sbuf("hid_bytes", [P, O], U8)
+        nc.vector.quantize_mx(out=hid_codes[:].bitcast(FP8X4), scales=hid_bytes[:],
+                              in_=hid[:].rearrange("p o t -> p (o t)"))
+        for h in range(N // P):
+            cols = slice(h * P, (h + 1) * P)
+            acc = psum_out.tile([P, O], F32, name="y_acc")
+            nc.tensor.matmul_mx(out=acc[:], lhsT=wb_codes[:, cols].bitcast(FP4X4), lhsT_scale=wb_plane[:, cols],
+                                rhs=hid_codes[:].bitcast(FP8X4), rhs_scale=hid_bytes[:], start=True, stop=True)
+            y = sbuf("y%d" % h, [P, O], F32)
+            if h == 0:
+                nc.vector.tensor_copy(y[:], acc[:])
+                nc.sync.dma_start(out[cols, :], y[:])
+            else:
+                nc.scalar.copy(y[:], acc[:])
+                nc.scalar.dma_start(out[cols, :], y[:])

@@ -57,12 +57,12 @@ def tile_picked_tokens_plain_two_staggered_one_plain_kernel(
         xt_plane = scale_plane("xt_plane", T)
         w_plane = scale_plane("w_plane", R)
 
-        put_a_list = load_list("put_a_list", offs3)
         tok_list = load_list("tok_list", offs)
         xt_table = load_words("xt_table", xt_words[0], T, U16)
-        w_raw = load_words("w_raw", w_words[0].rearrange("p n t -> p (n t)"), R, I32)
         load_scales(xt_plane, xt_scales)
+        w_raw = load_words("w_raw", w_words[0].rearrange("p n t -> p (n t)"), R, I32)
         load_scales(w_plane, w_scales)
+        put_a_list = load_list("put_a_list", offs3)
 
         board_w = [sbuf("board_w%d" % t, [P, C], F32) for t in range(PACK)]
         for t in range(PACK):
@@ -96,7 +96,7 @@ def tile_picked_tokens_plain_two_staggered_one_plain_kernel(
 
         nc.vector.tensor_copy(xt_bytes[:], xt_plane[:].indirect(tok_list[:]))
         nc.vector.tensor_copy(xt_codes[:], xt_table[:].indirect(tok_list[:]))
-        deal(w_codes, w_raw, 0, 1)
+        deal(w_codes, w_raw, 0, PACK)
         deal(w_bytes, w_plane, 0, 1)
 
         def product_to_board(name, codes, scales, moving, moving_scales, board, put_list):
@@ -104,7 +104,10 @@ def tile_picked_tokens_plain_two_staggered_one_plain_kernel(
             nc.tensor.matmul_mx(out=acc[:], lhsT=codes, lhsT_scale=scales, rhs=moving,
                                 rhs_scale=moving_scales, start=True, stop=True)
             res = sbuf(name, [P, J], F32)
-            nc.vector.tensor_copy(res[:], acc[:])
+            if name == "a0":
+                nc.scalar.activation(res[:], acc[:], COPY)
+            else:
+                nc.vector.tensor_copy(res[:], acc[:])
             nc.scalar.activation(board[:].indirect(put_list[:]), res[:], COPY)
 
         for t in range(PACK):
@@ -112,7 +115,6 @@ def tile_picked_tokens_plain_two_staggered_one_plain_kernel(
                              xt_codes[:].bitcast(FP4X4), xt_bytes[:], board_w[t], put_a_list)
             if t == 0:
                 deal(w_bytes, w_plane, 1, PACK)
-                deal(w_codes, w_raw, 1, PACK)
 
         xo_codes = sbuf("xo_codes", [P, J], U32)
         xo_bytes = sbuf("xo_bytes", [P, J], U8)
@@ -131,7 +133,7 @@ def tile_picked_tokens_plain_two_staggered_one_plain_kernel(
         hid = sbuf("hid", [P, O, PACK], BF16)
         fetched = []
         for t in range(PACK):
-            upper = sbuf("upper%d" % t, [P, C], F32)
+            upper = sbuf("upper%d" % t, [P, C], F32, tag="b%d" % t)
             lower = sbuf("lower%d" % t, [P, C], F32)
             nc.vector.tensor_scalar(upper[:, 0:1], board_w[t][:, 0:1], 0.0, None, ALU.max)
             nc.vector.tensor_tensor(upper[:, 1:C], board_w[t][:, 1:C], board_v[t][:, 0 : C - 1], ALU.max)

@@ -58,11 +58,11 @@ def tile_picked_tokens_plain_two_staggered_one_plain_kernel(
         w_plane = scale_plane("w_plane", R)
 
         tok_list = load_list("tok_list", offs)
+        put_a_list = load_list("put_a_list", offs3)
         xt_table = load_words("xt_table", xt_words[0], T, U16)
         load_scales(xt_plane, xt_scales)
         w_raw = load_words("w_raw", w_words[0].rearrange("p n t -> p (n t)"), R, I32)
         load_scales(w_plane, w_scales)
-        put_a_list = load_list("put_a_list", offs3)
 
         board_w = [sbuf("board_w%d" % t, [P, C], F32) for t in range(PACK)]
         for t in range(PACK):
@@ -94,8 +94,8 @@ def tile_picked_tokens_plain_two_staggered_one_plain_kernel(
         def deal(dst, src, t0, t1):
             nc.vector.tensor_copy(dst[:, t0:t1, :], src[:].rearrange("p (m t) -> p t m", t=PACK)[:, t0:t1, :])
 
-        nc.vector.tensor_copy(xt_bytes[:], xt_plane[:].indirect(tok_list[:]))
         nc.vector.tensor_copy(xt_codes[:], xt_table[:].indirect(tok_list[:]))
+        nc.vector.tensor_copy(xt_bytes[:], xt_plane[:].indirect(tok_list[:]))
         deal(w_codes, w_raw, 0, PACK)
         deal(w_bytes, w_plane, 0, 1)
 

@@ -104,10 +104,7 @@ def tile_picked_tokens_plain_two_staggered_one_plain_kernel(
             nc.tensor.matmul_mx(out=acc[:], lhsT=codes, lhsT_scale=scales, rhs=moving,
                                 rhs_scale=moving_scales, start=True, stop=True)
             res = sbuf(name, [P, J], F32)
-            if name == "a0":
-                nc.scalar.activation(res[:], acc[:], COPY)
-            else:
-                nc.vector.tensor_copy(res[:], acc[:])
+            nc.vector.tensor_copy(res[:], acc[:])
             nc.scalar.activation(board[:].indirect(put_list[:]), res[:], COPY)
 
         for t in range(PACK):
@@ -131,7 +128,8 @@ def tile_picked_tokens_plain_two_staggered_one_plain_kernel(
                              xo_codes[:].bitcast(FP8X4), xo_bytes[:], board_v[t], put_b_list)
 
         hid = sbuf("hid", [P, O, PACK], BF16)
-        fetched = []
+        hi = sbuf("hi", [P, PACK, O], F32)
+        lo = sbuf("lo", [P, PACK, O], F32)
         for t in range(PACK):
             upper = sbuf("upper%d" % t, [P, C], F32, tag="b%d" % t)
             lower = sbuf("lower%d" % t, [P, C], F32)
@@ -139,13 +137,15 @@ def tile_picked_tokens_plain_two_staggered_one_plain_kernel(
             nc.vector.tensor_tensor(upper[:, 1:C], board_w[t][:, 1:C], board_v[t][:, 0 : C - 1], ALU.max)
             nc.vector.tensor_scalar(lower[:, 0:1], board_v[t][:, 0:1], 0.0, None, ALU.min)
             nc.vector.tensor_tensor(lower[:, 1:C], board_v[t][:, 1:C], board_w[t][:, 0 : C - 1], ALU.min)
-            hi = sbuf("hi%d" % t, [P, O], F32)
-            lo = sbuf("lo%d" % t, [P, O], F32)
-            nc.scalar.activation(hi[:], upper[:].indirect(get_hi_list[:]), COPY, scale=sa_cols[:, t : t + 1])
-            nc.scalar.activation(lo[:], lower[:].indirect(get_lo_list[:]), COPY, scale=sb_cols[:, t : t + 1])
-            fetched.append((hi, lo))
-        for t, (hi, lo) in enumerate(fetched):
-            nc.vector.tensor_tensor(hid[:, :, t], hi[:], lo[:], ALU.subtract)
+            nc.scalar.activation(hi[:, t, :], upper[:].indirect(get_hi_list[:]), COPY, scale=sa_cols[:, t : t + 1])
+            nc.scalar.activation(lo[:, t, :], lower[:].indirect(get_lo_list[:]), COPY, scale=sb_cols[:, t : t + 1])
+        for t in range(0, PACK, 2):
+            nc.vector.tensor_tensor(
+                hid[:, :, t : t + 2],
+                hi[:, t : t + 2, :].rearrange("p t o -> p o t"),
+                lo[:, t : t + 2, :].rearrange("p t o -> p o t"),
+                ALU.subtract,
+            )
 
         hid_codes = sbuf("hid_codes", [P, O], U32)
         hid_bytes = sbuf("hid_bytes", [P, O], U8)

from contextlib import ExitStack

import concourse.mybir as mybir

K, J, R, T, Z, M, C, O, N = 512, 256, 512, 1024, 512, 1024, 512, 128, 256
FLOPS = 2 * (K * R * J + Z * R * J + R * N * O)

F32 = mybir.dt.float32
BF16 = mybir.dt.bfloat16
I32 = mybir.dt.int32
U32 = mybir.dt.uint32
U16 = mybir.dt.uint16
U8 = mybir.dt.uint8
FP8X4 = mybir.dt.float8_e4m3fn_x4
FP4X4 = mybir.dt.float4_e2m1fn_x4
COPY = mybir.ActivationFunctionType.Copy
ALU = mybir.AluOpType

P = 128
PACK = 4
QUADS = 4


def tile_picked_tokens_plain_two_staggered_one_plain_kernel(
    tc, xt_words, xt_scales, w_words, w_scales, xo_words, xo_scales, w2_words, w2_scales,
    sa, sb, wb_words, wb_scales, offs, offs2, offs3, offs4, offs5, offs6, out,
):
    nc = tc.nc
    with ExitStack() as ctx:
        keep = ctx.enter_context(tc.tile_pool(name="keep", bufs=1))
        psum = ctx.enter_context(tc.psum_pool(name="psum", bufs=4))
        psum_out = ctx.enter_context(tc.psum_pool(name="psum_out", bufs=2))

        def sbuf(name, shape, dtype, tag=None):
            return keep.tile(shape, dtype, name=name, tag=tag or name, align_bytes=64)

        def load_list(name, src):
            tile = sbuf(name, list(src.shape), U16)
            nc.sync.dma_start(tile[:], src)
            return tile

        def load_words(name, src, cols, dtype):
            tile = sbuf(name, [P, cols], dtype)
            nc.sync.dma_start(tile[:].bitcast(I32), src.bitcast(I32))
            return tile

        def scale_plane(name, cols):
            tile = sbuf(name, [P, cols], U8)
            nc.vector.memset(tile[:].bitcast(I32), 0)
            return tile

        def load_scales(plane, src):
            rows = src[0].bitcast(I32)
            for q in range(QUADS):
                nc.sync.dma_start(plane[32 * q : 32 * q + 4, :].bitcast(I32), rows[4 * q : 4 * q + 4, :])

        xt_plane = scale_plane("xt_plane", T)
        w_plane = scale_plane("w_plane", R)

        tok_list = load_list("tok_list", offs)
        put_a_list = load_list("put_a_list", offs3)
        xt_table = load_words("xt_table", xt_words[0], T, U16)
        load_scales(xt_plane, xt_scales)
        w_raw = load_words("w_raw", w_words[0].rearrange("p n t -> p (n t)"), R, I32)
        load_scales(w_plane, w_scales)

        board_w = [sbuf("board_w%d" % t, [P, C], F32) for t in range(PACK)]
        for t in range(PACK):
            nc.vector.memset(board_w[t][:], 0.0)

        xo_plane = scale_plane("xo_plane", M)
        w2_plane = scale_plane("w2_plane", R)
        wb_plane = sbuf("wb_plane", [P, N], U8)
        note_list = load_list("note_list", offs2)
        xo_table = load_words("xo_table", xo_words[0].rearrange("p n t -> p (n t)"), M, U32)
        load_scales(xo_plane, xo_scales)
        w2_raw = load_words("w2_raw", w2_words[0], R, U16)
        load_scales(w2_plane, w2_scales)
        put_b_list = load_list("put_b_list", offs4)
        sa_cols = sbuf("sa_cols", [P, PACK], F32)
        sb_cols = sbuf("sb_cols", [P, PACK], F32)
        nc.sync.dma_start(sa_cols[:], sa.rearrange("(p t) o -> p (t o)", t=PACK))
        nc.sync.dma_start(sb_cols[:], sb.rearrange("(p t) o -> p (t o)", t=PACK))
        get_hi_list = load_list("get_hi_list", offs5)
        get_lo_list = load_list("get_lo_list", offs6)
        wb_codes = load_words("wb_codes", wb_words[0], N, U16)
        load_scales(wb_plane, wb_scales)

        w_codes = sbuf("w_codes", [P, PACK, P], I32)
        w_bytes = sbuf("w_bytes", [P, PACK, P], U8)
        xt_codes = sbuf("xt_codes", [P, J], U16)
        xt_bytes = sbuf("xt_bytes", [P, J], U8)

        def deal(dst, src, t0, t1):
            nc.vector.tensor_copy(dst[:, t0:t1, :], src[:].rearrange("p (m t) -> p t m", t=PACK)[:, t0:t1, :])

        nc.vector.tensor_copy(xt_codes[:], xt_table[:].indirect(tok_list[:]))
        nc.vector.tensor_copy(xt_bytes[:], xt_plane[:].indirect(tok_list[:]))
        deal(w_codes, w_raw, 0, PACK)
        deal(w_bytes, w_plane, 0, 1)

        def product_to_board(name, codes, scales, moving, moving_scales, board, put_list):
            acc = psum.tile([P, J], F32, name="acc")
            nc.tensor.matmul_mx(out=acc[:], lhsT=codes, lhsT_scale=scales, rhs=moving,
                                rhs_scale=moving_scales, start=True, stop=True)
            res = sbuf(name, [P, J], F32)
            nc.vector.tensor_copy(res[:], acc[:])
            nc.scalar.activation(board[:].indirect(put_list[:]), res[:], COPY)

        for t in range(PACK):
            product_to_board("a%d" % t, w_codes[:, t, :].bitcast(FP8X4), w_bytes[:, t, :],
                             xt_codes[:].bitcast(FP4X4), xt_bytes[:], board_w[t], put_a_list)
            if t == 0:
                deal(w_bytes, w_plane, 1, PACK)

        xo_codes = sbuf("xo_codes", [P, J], U32)
        xo_bytes = sbuf("xo_bytes", [P, J], U8)
        w2_codes = sbuf("w2_codes", [P, PACK, P], U16)
        w2_bytes = sbuf("w2_bytes", [P, PACK, P], U8)
        nc.vector.tensor_copy(xo_codes[:], xo_table[:].indirect(note_list[:]))
        nc.vector.tensor_copy(xo_bytes[:], xo_plane[:].indirect(note_list[:]))
        deal(w2_codes, w2_raw, 0, PACK)
        deal(w2_bytes, w2_plane, 0, PACK)
        board_v = [sbuf("board_v%d" % t, [P, C], F32, tag="a%d" % t) for t in range(PACK)]
        for t in range(PACK):
            nc.gpsimd.memset(board_v[t][:], 0.0)
            product_to_board("b%d" % t, w2_codes[:, t, :].bitcast(FP4X4), w2_bytes[:, t, :],
                             xo_codes[:].bitcast(FP8X4), xo_bytes[:], board_v[t], put_b_list)

        hid = sbuf("hid", [P, O, PACK], BF16)
        hi = sbuf("hi", [P, PACK, O], F32)
        lo = sbuf("lo", [P, PACK, O], F32)
        for t in range(PACK):
            upper = sbuf("upper%d" % t, [P, C], F32, tag="b%d" % t)
            lower = sbuf("lower%d" % t, [P, C], F32)
            nc.vector.tensor_scalar(upper[:, 0:1], board_w[t][:, 0:1], 0.0, None, ALU.max)
            nc.vector.tensor_tensor(upper[:, 1:C], board_w[t][:, 1:C], board_v[t][:, 0 : C - 1], ALU.max)
            nc.vector.tensor_scalar(lower[:, 0:1], board_v[t][:, 0:1], 0.0, None, ALU.min)
            nc.vector.tensor_tensor(lower[:, 1:C], board_v[t][:, 1:C], board_w[t][:, 0 : C - 1], ALU.min)
            nc.scalar.activation(hi[:, t, :], upper[:].indirect(get_hi_list[:]), COPY, scale=sa_cols[:, t : t + 1])
            nc.scalar.activation(lo[:, t, :], lower[:].indirect(get_lo_list[:]), COPY, scale=sb_cols[:, t : t + 1])
        for t in range(0, PACK, 2):
            nc.vector.tensor_tensor(
                hid[:, :, t : t + 2],
                hi[:, t : t + 2, :].rearrange("p t o -> p o t"),
                lo[:, t : t + 2, :].rearrange("p t o -> p o t"),
                ALU.subtract,
            )

        hid_codes = sbuf("hid_codes", [P, O], U32)
        hid_bytes = sbuf("hid_bytes", [P, O], U8)
        nc.vector.quantize_mx(out=hid_codes[:].bitcast(FP8X4), scales=hid_bytes[:],
                              in_=hid[:].rearrange("p o t -> p (o t)"))
        for h in range(N // P):
            cols = slice(h * P, (h + 1) * P)
            acc = psum_out.tile([P, O], F32, name="y_acc")
            nc.tensor.matmul_mx(out=acc[:], lhsT=wb_codes[:, cols].bitcast(FP4X4), lhsT_scale=wb_plane[:, cols],
                                rhs=hid_codes[:].bitcast(FP8X4), rhs_scale=hid_bytes[:], start=True, stop=True)
            y = sbuf("y%d" % h, [P, O], F32)
            if h == 0:
                nc.vector.tensor_copy(y[:], acc[:])
                nc.sync.dma_start(out[cols, :], y[:])
            else:
                nc.scalar.copy(y[:], acc[:])
                nc.scalar.dma_start(out[cols, :], y[:])
